import numpy as np
import ml_dtypes

BF16 = ml_dtypes.bfloat16


def bf(x):
    return np.asarray(x, np.float32).astype(BF16)


def f32(x):
    return np.asarray(x, np.float32)


def f64(x):
    return np.asarray(x).astype(np.float64)


def striped(idx):
    return np.tile(idx.reshape(-1, 16).T, (8, 1))


S, K, M, N, E, Q = 2048, 256, 128, 4096, 8, 512


def gelu_tanh(v):
    return 0.5 * v * (1.0 + np.tanh(np.sqrt(2.0 / np.pi) * (v + 0.044715 * v**3)))


def two_experts():
    first = np.random.permutation(S).reshape(E, S // E)
    return np.concatenate([np.random.permutation(np.concatenate([first[e], first[(e + 1) % E]])) for e in range(E)])


def setup_inputs():
    return {"table": bf(np.random.standard_normal((K, S))), "w": bf(np.random.standard_normal((E, K, M)) / np.sqrt(K)), "b": f32(0.5 * np.random.standard_normal((M, 1))), "offs": striped(two_experts())}


def reference(table, w, b, offs):
    idx = offs[:16].T.reshape(-1)
    x = f64(table)[:, idx]
    y = np.concatenate([f64(w)[e].T @ x[:, e * Q : (e + 1) * Q] for e in range(E)], axis=1)
    return gelu_tanh(y + f64(b))

@@ -1,0 +1,64 @@
+import concourse.mybir as mybir
+
+BF16 = mybir.dt.bfloat16
+F32 = mybir.dt.float32
+U16 = mybir.dt.uint16
+ACT = mybir.ActivationFunctionType
+
+P = 128
+K = 256
+BLOCKS = K // P
+S = 2048
+M = 128
+E = 8
+Q = 512
+N = E * Q
+
+FLOPS = 2 * K * M * N
+
+
+def tile_gather_matmul_kernel(tc, table, w, b, offs, out):
+    nc = tc.nc
+    table_rows = table.rearrange("(p t) s -> p t s", t=BLOCKS)
+    w_rows = w.rearrange("e (p t) m -> p e (t m)", t=BLOCKS)
+    half = E // 2
+
+    with (
+        tc.tile_pool(name="held", bufs=1) as held,
+        tc.tile_pool(name="results", bufs=E) as results,
+        tc.psum_pool(name="banks", bufs=E) as banks,
+    ):
+        offsets = held.tile([P, N // 16], U16, name="offsets")
+        blocks = [held.tile([P, S], BF16, name=f"block{t}") for t in range(BLOCKS)]
+        weights = [held.tile([P, half, BLOCKS * M], BF16, name=f"weights{h}") for h in range(2)]
+        bias = held.tile([P, 1], F32, name="bias")
+
+        nc.scalar.dma_start(weights[0][:], w_rows[:, 0:half, :])
+        nc.sync.dma_start(offsets[:], offs)
+        nc.sync.dma_start(blocks[0][:], table_rows[:, 0, :])
+        nc.sync.dma_start(blocks[1][:], table_rows[:, 1, :])
+        nc.sync.dma_start(weights[1][:], w_rows[:, half:E, :])
+        nc.scalar.dma_start(bias[:], b)
+
+        zero = held.tile([P, 1], F32, name="zero")
+        warm = held.tile([P, 1], F32, name="warm")
+        nc.vector.memset(zero[:], 0.0)
+        nc.scalar.activation(warm[:], zero[:], ACT.Gelu_apprx_tanh)
+
+        for h in range(2):
+            experts = range(h * half, (h + 1) * half)
+            sums = {e: banks.tile([P, Q], F32, name=f"sum{e}", tag="sum") for e in experts}
+            for t in range(BLOCKS):
+                for e in experts:
+                    picked = blocks[t][:].indirect(offsets[:, e * (Q // 16) : (e + 1) * (Q // 16)])
+                    nc.tensor.matmul(
+                        sums[e][:],
+                        weights[h][:, e - h * half, t * M : (t + 1) * M],
+                        picked,
+                        start=t == 0,
+                        stop=t == BLOCKS - 1,
+                    )
+            for e in experts:
+                result = results.tile([P, Q], F32, name="result")
+                nc.scalar.activation(result[:], sums[e][:], ACT.Gelu_apprx_tanh, bias=bias[:, 0:1])
+                nc.sync.dma_start(out[:, e * Q : (e + 1) * Q], result[:])

@@ -21,7 +21,7 @@ def tile_gather_matmul_kernel(tc, table, w, b, offs, out):
     nc = tc.nc
     table_rows = table.rearrange("(p t) s -> p t s", t=BLOCKS)
     w_rows = w.rearrange("e (p t) m -> p e (t m)", t=BLOCKS)
-    half = E // 2
+    groups = [range(0, 2), range(2, E)]
 
     with (
         tc.tile_pool(name="held", bufs=1) as held,
@@ -30,14 +30,14 @@ def tile_gather_matmul_kernel(tc, table, w, b, offs, out):
     ):
         offsets = held.tile([P, N // 16], U16, name="offsets")
         blocks = [held.tile([P, S], BF16, name=f"block{t}") for t in range(BLOCKS)]
-        weights = [held.tile([P, half, BLOCKS * M], BF16, name=f"weights{h}") for h in range(2)]
+        weights = [held.tile([P, len(g), BLOCKS * M], BF16, name=f"weights{g[0]}") for g in groups]
         bias = held.tile([P, 1], F32, name="bias")
 
-        nc.scalar.dma_start(weights[0][:], w_rows[:, 0:half, :])
+        nc.scalar.dma_start(weights[0][:], w_rows[:, 0 : len(groups[0]), :])
         nc.sync.dma_start(offsets[:], offs)
         nc.sync.dma_start(blocks[0][:], table_rows[:, 0, :])
         nc.sync.dma_start(blocks[1][:], table_rows[:, 1, :])
-        nc.sync.dma_start(weights[1][:], w_rows[:, half:E, :])
+        nc.sync.dma_start(weights[1][:], w_rows[:, len(groups[0]) : E, :])
         nc.scalar.dma_start(bias[:], b)
 
         zero = held.tile([P, 1], F32, name="zero")
@@ -45,20 +45,19 @@ def tile_gather_matmul_kernel(tc, table, w, b, offs, out):
         nc.vector.memset(zero[:], 0.0)
         nc.scalar.activation(warm[:], zero[:], ACT.Gelu_apprx_tanh)
 
-        for h in range(2):
-            experts = range(h * half, (h + 1) * half)
-            sums = {e: banks.tile([P, Q], F32, name=f"sum{e}", tag="sum") for e in experts}
-            for t in range(BLOCKS):
-                for e in experts:
-                    picked = blocks[t][:].indirect(offsets[:, e * (Q // 16) : (e + 1) * (Q // 16)])
-                    nc.tensor.matmul(
-                        sums[e][:],
-                        weights[h][:, e - h * half, t * M : (t + 1) * M],
-                        picked,
-                        start=t == 0,
-                        stop=t == BLOCKS - 1,
-                    )
-            for e in experts:
+        sums = [banks.tile([P, Q], F32, name=f"sum{e}", tag="sum") for e in range(E)]
+        order = [(e, t) for t in range(BLOCKS) for e in groups[0]]
+        order += [(e, t) for e in groups[1] for t in range(BLOCKS)]
+        for e, t in order:
+            g = 0 if e in groups[0] else 1
+            nc.tensor.matmul(
+                sums[e][:],
+                weights[g][:, e - groups[g][0], t * M : (t + 1) * M],
+                blocks[t][:].indirect(offsets[:, e * (Q // 16) : (e + 1) * (Q // 16)]),
+                start=t == 0,
+                stop=t == BLOCKS - 1,
+            )
+            if t == BLOCKS - 1:
                 result = results.tile([P, Q], F32, name="result")
                 nc.scalar.activation(result[:], sums[e][:], ACT.Gelu_apprx_tanh, bias=bias[:, 0:1])
                 nc.sync.dma_start(out[:, e * Q : (e + 1) * Q], result[:])

@@ -21,7 +21,7 @@ def tile_gather_matmul_kernel(tc, table, w, b, offs, out):
     nc = tc.nc
     table_rows = table.rearrange("(p t) s -> p t s", t=BLOCKS)
     w_rows = w.rearrange("e (p t) m -> p e (t m)", t=BLOCKS)
-    groups = [range(0, 2), range(2, E)]
+    pairs = E // 2
 
     with (
         tc.tile_pool(name="held", bufs=1) as held,
@@ -30,14 +30,15 @@ def tile_gather_matmul_kernel(tc, table, w, b, offs, out):
     ):
         offsets = held.tile([P, N // 16], U16, name="offsets")
         blocks = [held.tile([P, S], BF16, name=f"block{t}") for t in range(BLOCKS)]
-        weights = [held.tile([P, len(g), BLOCKS * M], BF16, name=f"weights{g[0]}") for g in groups]
+        weights = [held.tile([P, 2, BLOCKS * M], BF16, name=f"weights{i}") for i in range(pairs)]
         bias = held.tile([P, 1], F32, name="bias")
 
-        nc.scalar.dma_start(weights[0][:], w_rows[:, 0 : len(groups[0]), :])
+        nc.scalar.dma_start(weights[0][:], w_rows[:, 0:2, :])
         nc.sync.dma_start(offsets[:], offs)
         nc.sync.dma_start(blocks[0][:], table_rows[:, 0, :])
         nc.sync.dma_start(blocks[1][:], table_rows[:, 1, :])
-        nc.sync.dma_start(weights[1][:], w_rows[:, len(groups[0]) : E, :])
+        for i in range(1, pairs):
+            nc.sync.dma_start(weights[i][:], w_rows[:, 2 * i : 2 * i + 2, :])
         nc.scalar.dma_start(bias[:], b)
 
         zero = held.tile([P, 1], F32, name="zero")
@@ -46,13 +47,12 @@ def tile_gather_matmul_kernel(tc, table, w, b, offs, out):
         nc.scalar.activation(warm[:], zero[:], ACT.Gelu_apprx_tanh)
 
         sums = [banks.tile([P, Q], F32, name=f"sum{e}", tag="sum") for e in range(E)]
-        order = [(e, t) for t in range(BLOCKS) for e in groups[0]]
-        order += [(e, t) for e in groups[1] for t in range(BLOCKS)]
+        order = [(e, t) for t in range(BLOCKS) for e in range(2)]
+        order += [(e, t) for e in range(2, E) for t in range(BLOCKS)]
         for e, t in order:
-            g = 0 if e in groups[0] else 1
             nc.tensor.matmul(
                 sums[e][:],
-                weights[g][:, e - groups[g][0], t * M : (t + 1) * M],
+                weights[e // 2][:, e % 2, t * M : (t + 1) * M],
                 blocks[t][:].indirect(offsets[:, e * (Q // 16) : (e + 1) * (Q // 16)]),
                 start=t == 0,
                 stop=t == BLOCKS - 1,

import concourse.mybir as mybir

BF16 = mybir.dt.bfloat16
F32 = mybir.dt.float32
U16 = mybir.dt.uint16
ACT = mybir.ActivationFunctionType

P = 128
K = 256
BLOCKS = K // P
S = 2048
M = 128
E = 8
Q = 512
N = E * Q

FLOPS = 2 * K * M * N


def tile_gather_matmul_kernel(tc, table, w, b, offs, out):
    nc = tc.nc
    table_rows = table.rearrange("(p t) s -> p t s", t=BLOCKS)
    w_rows = w.rearrange("e (p t) m -> p e (t m)", t=BLOCKS)
    pairs = E // 2

    with (
        tc.tile_pool(name="held", bufs=1) as held,
        tc.tile_pool(name="results", bufs=E) as results,
        tc.psum_pool(name="banks", bufs=E) as banks,
    ):
        offsets = held.tile([P, N // 16], U16, name="offsets")
        blocks = [held.tile([P, S], BF16, name=f"block{t}") for t in range(BLOCKS)]
        weights = [held.tile([P, 2, BLOCKS * M], BF16, name=f"weights{i}") for i in range(pairs)]
        bias = held.tile([P, 1], F32, name="bias")

        nc.scalar.dma_start(weights[0][:], w_rows[:, 0:2, :])
        nc.sync.dma_start(offsets[:], offs)
        nc.sync.dma_start(blocks[0][:], table_rows[:, 0, :])
        nc.sync.dma_start(blocks[1][:], table_rows[:, 1, :])
        for i in range(1, pairs):
            nc.sync.dma_start(weights[i][:], w_rows[:, 2 * i : 2 * i + 2, :])
        nc.scalar.dma_start(bias[:], b)

        zero = held.tile([P, 1], F32, name="zero")
        warm = held.tile([P, 1], F32, name="warm")
        nc.vector.memset(zero[:], 0.0)
        nc.scalar.activation(warm[:], zero[:], ACT.Gelu_apprx_tanh)

        sums = [banks.tile([P, Q], F32, name=f"sum{e}", tag="sum") for e in range(E)]
        order = [(e, t) for t in range(BLOCKS) for e in range(2)]
        order += [(e, t) for e in range(2, E) for t in range(BLOCKS)]
        for e, t in order:
            nc.tensor.matmul(
                sums[e][:],
                weights[e // 2][:, e % 2, t * M : (t + 1) * M],
                blocks[t][:].indirect(offsets[:, e * (Q // 16) : (e + 1) * (Q // 16)]),
                start=t == 0,
                stop=t == BLOCKS - 1,
            )
            if t == BLOCKS - 1:
                result = results.tile([P, Q], F32, name="result")
                nc.scalar.activation(result[:], sums[e][:], ACT.Gelu_apprx_tanh, bias=bias[:, 0:1])
                nc.sync.dma_start(out[:, e * Q : (e + 1) * Q], result[:])
